import numpy as np
import ml_dtypes


def mxq(x, axis, fmt="e4m3"):
    dtype, down = {"e4m3": (ml_dtypes.float8_e4m3fn, 7), "e5m2": (ml_dtypes.float8_e5m2, 14)}[fmt]
    v = np.moveaxis(np.asarray(x, np.float32).astype(ml_dtypes.bfloat16).astype(np.float64), axis, -1)
    blocks = v.reshape(v.shape[:-1] + (-1, 32))
    amax = np.abs(blocks).max(-1, keepdims=True)
    byte = np.maximum(np.where(amax > 0, np.frexp(amax)[1] - 1 + 127, 0) - down, 1)
    scale = np.exp2(byte - 127.0)
    codes = (blocks / scale).astype(np.float32).astype(dtype).astype(np.float64)
    return np.moveaxis((codes * scale).reshape(v.shape), -1, axis)


WIDE = False


def mx_kscale(k):
    if not WIDE:
        return np.ones(k)
    levels = np.array([30, -30])
    if k % 512:
        return np.exp2(np.random.permutation(np.resize(levels, k // 32))).repeat(32)
    a = np.empty((k // 512, 16))
    for p in range(k // 512):
        a[p, :8] = np.random.permutation(np.resize(levels, 8))
        for g in range(8):
            far = levels[np.abs(levels - a[p, g]) >= 10]
            a[p, g + 8] = far[np.random.randint(len(far))]
    return np.exp2(a.ravel()).repeat(32)


def f64(x):
    return np.asarray(x).astype(np.float64)


def striped(idx):
    return np.tile(np.asarray(idx).reshape(-1, 16).T, (8, 1)).astype(np.uint16)


def unstriped(offs):
    return offs[:16].T.reshape(-1).astype(np.int64)


E2M1 = np.array([0.0, 0.5, 1.0, 1.5, 2.0, 3.0, 4.0, 6.0, -0.0, -0.5, -1.0, -1.5, -2.0, -3.0, -4.0, -6.0])


def pack_weight(w, fmt):
    k, n = w.shape
    w = f64(np.asarray(w, np.float32).astype(ml_dtypes.bfloat16)).reshape(k // 32, 32, n)
    amax = np.abs(w).max(1)
    if fmt == "e4m3":
        byte = np.frexp(amax)[1] - 1 + 127 - 7
    else:
        mant, ex = np.frexp(amax / 6.0)
        byte = np.where(mant > 0.5, ex, ex - 1) + 127
    byte = np.clip(np.where(amax > 0, byte, 1), 1, 254)
    scaled = (w * np.exp2(127.0 - byte)[:, None, :]).reshape(k, n).astype(np.float32)
    by_word = np.ascontiguousarray(scaled.reshape(k // 512, 128, 4, n).transpose(0, 1, 3, 2))
    if fmt == "e4m3":
        words = by_word.astype(ml_dtypes.float8_e4m3fn).view(np.uint8)
    else:
        c = by_word.astype(ml_dtypes.float4_e2m1fn).view(np.uint8) & 0xF
        words = (c[..., 0::2] | (c[..., 1::2] << 4)).reshape(k // 512, 128, 2 * n)
    return np.ascontiguousarray(words), np.ascontiguousarray(byte.astype(np.uint8).reshape(k // 512, 16, n))


def unpack_weight(words, scales, fmt):
    g, _, n = scales.shape
    words = np.ascontiguousarray(words).reshape(g, 128, n, -1)
    if fmt == "e4m3":
        vals = words.view(ml_dtypes.float8_e4m3fn).astype(np.float64)
    else:
        nib = np.empty((g, 128, n, 4), np.uint8)
        nib[..., 0::2] = words & 0xF
        nib[..., 1::2] = words >> 4
        vals = E2M1[nib]
    vals = vals * np.repeat(np.exp2(scales.astype(np.float64) - 127.0), 8, axis=1)[..., None]
    return vals.transpose(0, 1, 3, 2).reshape(g * 512, n)


def sigmoid(v):
    return 1.0 / (1.0 + np.exp(-v))


K, T, J, R, O, N, L, E = 512, 2048, 256, 512, 128, 256, 512, 512


def setup_inputs():
    n = np.random.standard_normal
    idx = np.random.permutation(T)[:J]
    idx2 = np.random.permutation(T)[:J]
    idx3 = np.random.permutation(T)[:J]
    idx4 = np.random.permutation(J)[:O]
    idx5 = np.random.permutation(J)[:O]
    idx6 = np.random.permutation(E)[:O]
    fk = mx_kscale(K)
    fr = mx_kscale(R)
    fl = mx_kscale(L)
    xtp = pack_weight(n((K, T)) / fk[:, None], "e2m1")
    wp = pack_weight(n((K, R)) * 1 / np.sqrt(K) * fk[:, None] * fr, "e4m3")
    wbp = pack_weight(n((R, N)) * 1 / np.sqrt(R) / fr[:, None], "e2m1")
    sxp = pack_weight(n((L, O)) / fl[:, None], "e4m3")
    wsp = pack_weight(n((L, N)) * 1 / np.sqrt(L) * fl[:, None], "e4m3")
    return {
        "xt_words": xtp[0],
        "xt_scales": xtp[1],
        "w_words": wp[0],
        "w_scales": wp[1],
        "wb_words": wbp[0],
        "wb_scales": wbp[1],
        "sx_words": sxp[0],
        "sx_scales": sxp[1],
        "ws_words": wsp[0],
        "ws_scales": wsp[1],
        "tz": (n((N, E))).astype(np.float32),
        "so": (np.random.uniform(0.6, 1.6, (N, 1))).astype(np.float32),
        "bo": (np.random.uniform(-1.0, 1.0, (N, 1))).astype(np.float32),
        "offs": striped(idx),
        "offs2": striped(idx2),
        "offs3": striped(idx3),
        "offs4": striped(idx4),
        "offs5": striped(idx5),
        "offs6": striped(idx6),
    }


def reference(xt_words, xt_scales, w_words, w_scales, wb_words, wb_scales, sx_words, sx_scales, ws_words, ws_scales, tz, so, bo, offs, offs2, offs3, offs4, offs5, offs6):
    idx = unstriped(offs)
    idx2 = unstriped(offs2)
    idx3 = unstriped(offs3)
    idx4 = unstriped(offs4)
    idx5 = unstriped(offs5)
    idx6 = unstriped(offs6)
    xtu = unpack_weight(xt_words, xt_scales, "e2m1")
    wu = unpack_weight(w_words, w_scales, "e4m3")
    wbu = unpack_weight(wb_words, wb_scales, "e2m1")
    sxu = unpack_weight(sx_words, sx_scales, "e4m3")
    wsu = unpack_weight(ws_words, ws_scales, "e4m3")
    xtidxg = xtu[:, idx]
    a = wu.T @ xtidxg
    xtidx2g = xtu[:, idx2]
    b = wu.T @ xtidx2g
    xtidx3g = xtu[:, idx3]
    g0 = wu.T @ xtidx3g
    c1 = np.maximum(b, g0)
    hid = np.abs(a[:, idx4] - c1[:, idx5])
    hidq = mxq(hid, 0, "e5m2")
    p = wbu.T @ hidq + wsu.T @ sxu
    y = p * sigmoid(f64(tz)[:, idx6] * f64(so) + f64(bo))
    return y

@@ -1,0 +1,163 @@
+from contextlib import ExitStack
+
+import concourse.mybir as mybir
+
+K, T, J, R, O, N, L, E = 512, 2048, 256, 512, 128, 256, 512, 512
+FLOPS = 2 * K * R * 3 * J + 2 * R * N * O + 2 * L * N * O
+
+F32 = mybir.dt.float32
+BF16 = mybir.dt.bfloat16
+I32 = mybir.dt.int32
+U32 = mybir.dt.uint32
+U16 = mybir.dt.uint16
+U8 = mybir.dt.uint8
+E4M3 = mybir.dt.float8_e4m3fn_x4
+E5M2 = mybir.dt.float8_e5m2_x4
+E2M1 = mybir.dt.float4_e2m1fn_x4
+ACT = mybir.ActivationFunctionType
+ALU = mybir.AluOpType
+
+P = 128
+PACK = 4
+HALVES = N // P
+
+
+def load_scale_rows(nc, plane, scales):
+    for q in range(4):
+        rows = scales[0, 4 * q : 4 * q + 4, :].bitcast(I32)
+        nc.sync.dma_start(out=plane[32 * q : 32 * q + 32, :].bitcast(I32), in_=rows.unsqueeze(0).to_broadcast([8] + list(rows.shape)))
+
+
+def tile_list_triple_looked_skip_finalgate_kernel(
+    tc, xt_words, xt_scales, w_words, w_scales, wb_words, wb_scales, sx_words, sx_scales, ws_words, ws_scales,
+    tz, so, bo, offs, offs2, offs3, offs4, offs5, offs6, out,
+):
+    nc = tc.nc
+    with ExitStack() as ctx:
+        sb = ctx.enter_context(tc.tile_pool(name="sb", bufs=1))
+        ps = ctx.enter_context(tc.psum_pool(name="ps", bufs=1))
+
+        def tile(name, shape, dtype):
+            return sb.tile(shape, dtype, name=name, align_bytes=64)
+
+        def load_list(name, source):
+            offsets = tile(name, list(source.shape), U16)
+            nc.sync.dma_start(offsets[:], source)
+            return offsets
+
+        def load_words(name, source, width):
+            words = tile(name, [P, width], U32)
+            nc.sync.dma_start(out=words[:].bitcast(I32), in_=source[0].rearrange("p c r -> p (c r)").bitcast(I32))
+            return words
+
+        w_plane = tile("w_plane", [P, R], U8)
+        xt_plane = tile("xt_plane", [P, T], U8)
+        ws_plane = tile("ws_plane", [P, N], U8)
+        sx_plane = tile("sx_plane", [P, O], U8)
+        wb_plane = tile("wb_plane", [P, N], U8)
+
+        nc.vector.memset(xt_plane[:].bitcast(I32), 0)
+        w_codes = load_words("w_codes", w_words, R)
+        list_a = load_list("list_a", offs)
+        list_b = load_list("list_b", offs2)
+        load_scale_rows(nc, w_plane, w_scales)
+        xt_codes = tile("xt_codes", [P, T], U16)
+        nc.sync.dma_start(out=xt_codes[:].bitcast(I32), in_=xt_words[0].bitcast(I32))
+        for q in range(4):
+            nc.sync.dma_start(out=xt_plane[32 * q : 32 * q + 4, :].bitcast(I32), in_=xt_scales[0, 4 * q : 4 * q + 4, :].bitcast(I32))
+        slope = tile("slope", [P, HALVES], F32)
+        offset = tile("offset", [P, HALVES], F32)
+        with nc.allow_non_contiguous_dma(reason="one value a partition"):
+            nc.sync.dma_start(out=slope[:], in_=so.rearrange("(h p) one -> p (h one)", p=P))
+            nc.sync.dma_start(out=offset[:], in_=bo.rearrange("(h p) one -> p (h one)", p=P))
+        gate_table = [sb.tile([P, E], F32, name="gate_table%d" % h, tag="wide%d" % h, align_bytes=64) for h in range(HALVES)]
+        nc.sync.dma_start(out=gate_table[0][:], in_=tz[0:P, :])
+        list_gate = load_list("list_gate", offs6)
+        list_g = load_list("list_g", offs3)
+        nc.sync.dma_start(out=gate_table[1][:], in_=tz[P : 2 * P, :])
+        pick_a = load_list("pick_a", offs4)
+        pick_c = load_list("pick_c", offs5)
+        ws_codes = load_words("ws_codes", ws_words, N)
+        sx_codes = load_words("sx_codes", sx_words, O)
+        load_scale_rows(nc, ws_plane, ws_scales)
+        load_scale_rows(nc, sx_plane, sx_scales)
+        wb_codes = tile("wb_codes", [P, N], U16)
+        nc.sync.dma_start(out=wb_codes[:].bitcast(I32), in_=wb_words[0].bitcast(I32))
+        load_scale_rows(nc, wb_plane, wb_scales)
+
+        w_codes_t = tile("w_codes_t", [P, PACK, P], U32)
+        w_plane_t = tile("w_plane_t", [P, PACK, P], U8)
+        nc.vector.tensor_copy(out=w_codes_t[:].rearrange("p t m -> p m t"), in_=w_codes[:].rearrange("p (m t) -> p m t", t=PACK))
+        nc.vector.tensor_copy(out=w_plane_t[:].rearrange("p t m -> p m t"), in_=w_plane[:].rearrange("p (m t) -> p m t", t=PACK))
+
+        gate = [tile("gate%d" % h, [P, O], F32) for h in range(HALVES)]
+        for h in range(HALVES):
+            nc.scalar.activation(
+                out=gate[h][:], in_=gate_table[h][:].indirect(list_gate[:]), func=ACT.Sigmoid,
+                bias=offset[:, h : h + 1], scale=slope[:, h : h + 1],
+            )
+
+        def first_product(name, offsets):
+            codes = tile(name + "_codes", [P, J], U16)
+            plane = tile(name + "_plane", [P, J], U8)
+            nc.vector.tensor_copy(out=codes[:], in_=xt_codes[:].indirect(offsets[:]))
+            nc.vector.tensor_copy(out=plane[:], in_=xt_plane[:].indirect(offsets[:]))
+            banks = [ps.tile([P, 2, J], F32, name="%s_bank%d" % (name, u)) for u in range(2)]
+            for t in range(PACK):
+                nc.tensor.matmul_mx(
+                    out=banks[t // 2][:, t % 2, :],
+                    lhsT=w_codes_t[:, t, :].bitcast(E4M3), lhsT_scale=w_plane_t[:, t, :],
+                    rhs=codes[:].bitcast(E2M1), rhs_scale=plane[:],
+                    start=True, stop=True,
+                )
+            return banks
+
+        def to_sbuf(name, banks, tags):
+            pairs = [sb.tile([P, 2, J], F32, name="%s_pair%d" % (name, u), tag=tags[u], align_bytes=64) for u in range(2)]
+            for u in range(2):
+                nc.scalar.copy(out=pairs[u][:], in_=banks[u][:])
+            return pairs
+
+        a_pairs = to_sbuf("a", first_product("a", list_a), ("wide0", "a_pair1"))
+        b_pairs = to_sbuf("b", first_product("b", list_b), ("b_pair0", "b_pair1"))
+        g_banks = first_product("g", list_g)
+
+        sums = [ps.tile([P, O], F32, name="sum%d" % h) for h in range(HALVES)]
+        for h in range(HALVES):
+            nc.tensor.matmul_mx(
+                out=sums[h][:],
+                lhsT=ws_codes[:, h * P : (h + 1) * P].bitcast(E4M3), lhsT_scale=ws_plane[:, h * P : (h + 1) * P],
+                rhs=sx_codes[:].bitcast(E4M3), rhs_scale=sx_plane[:],
+                start=True, stop=False,
+            )
+
+        a_picked = [tile("a_picked%d" % t, [P, O], F32) for t in range(PACK)]
+        for t in range(PACK):
+            nc.scalar.activation(out=a_picked[t][:], in_=a_pairs[t // 2][:, t % 2, :].indirect(pick_a[:]), func=ACT.Copy)
+
+        larger = [tile("larger%d" % t, [P, J], F32) for t in range(PACK)]
+        for t in range(PACK):
+            nc.vector.tensor_tensor(out=larger[t][:], in0=g_banks[t // 2][:, t % 2, :], in1=b_pairs[t // 2][:, t % 2, :], op=ALU.max)
+        diff = tile("diff", [P, PACK, O], F32)
+        for t in range(PACK):
+            nc.vector.tensor_tensor(out=diff[:, t, :], in0=larger[t][:].indirect(pick_c[:]), in1=a_picked[t][:], op=ALU.subtract)
+
+        hid = tile("hid", [P, O, PACK], BF16)
+        nc.scalar.activation(
+            out=hid[:].rearrange("p (c i) t -> p c t i", i=4), in_=diff[:].rearrange("p t (c i) -> p c t i", i=4), func=ACT.Abs,
+        )
+        hid_codes = tile("hid_codes", [P, O], U32)
+        hid_plane = tile("hid_plane", [P, O], U8)
+        nc.vector.quantize_mx(out=hid_codes[:].bitcast(E5M2), scales=hid_plane[:], in_=hid[:].rearrange("p o t -> p (o t)"))
+
+        for h in range(HALVES):
+            nc.tensor.matmul_mx(
+                out=sums[h][:],
+                lhsT=wb_codes[:, h * P : (h + 1) * P].bitcast(E2M1), lhsT_scale=wb_plane[:, h * P : (h + 1) * P],
+                rhs=hid_codes[:].bitcast(E5M2), rhs_scale=hid_plane[:],
+                start=False, stop=True,
+            )
+            result = tile("result%d" % h, [P, O], F32)
+            nc.vector.tensor_tensor(out=result[:], in0=sums[h][:], in1=gate[h][:], op=ALU.mult)
+            queue = nc.sync if h == 0 else nc.scalar
+            queue.dma_start(out=out[h * P : (h + 1) * P, :], in_=result[:])

@@ -22,8 +22,8 @@ PACK = 4
 HALVES = N // P
 
 
-def load_scale_rows(nc, plane, scales):
-    for q in range(4):
+def load_scale_rows(nc, plane, scales, quadrants=range(4)):
+    for q in quadrants:
         rows = scales[0, 4 * q : 4 * q + 4, :].bitcast(I32)
         nc.sync.dma_start(out=plane[32 * q : 32 * q + 32, :].bitcast(I32), in_=rows.unsqueeze(0).to_broadcast([8] + list(rows.shape)))
 
@@ -57,24 +57,16 @@ def tile_list_triple_looked_skip_finalgate_kernel(
         wb_plane = tile("wb_plane", [P, N], U8)
 
         nc.vector.memset(xt_plane[:].bitcast(I32), 0)
+        load_scale_rows(nc, w_plane, w_scales, range(3))
         w_codes = load_words("w_codes", w_words, R)
-        list_a = load_list("list_a", offs)
-        list_b = load_list("list_b", offs2)
-        load_scale_rows(nc, w_plane, w_scales)
+        load_scale_rows(nc, w_plane, w_scales, range(3, 4))
         xt_codes = tile("xt_codes", [P, T], U16)
         nc.sync.dma_start(out=xt_codes[:].bitcast(I32), in_=xt_words[0].bitcast(I32))
+        list_a = load_list("list_a", offs)
         for q in range(4):
             nc.sync.dma_start(out=xt_plane[32 * q : 32 * q + 4, :].bitcast(I32), in_=xt_scales[0, 4 * q : 4 * q + 4, :].bitcast(I32))
-        slope = tile("slope", [P, HALVES], F32)
-        offset = tile("offset", [P, HALVES], F32)
-        with nc.allow_non_contiguous_dma(reason="one value a partition"):
-            nc.sync.dma_start(out=slope[:], in_=so.rearrange("(h p) one -> p (h one)", p=P))
-            nc.sync.dma_start(out=offset[:], in_=bo.rearrange("(h p) one -> p (h one)", p=P))
-        gate_table = [sb.tile([P, E], F32, name="gate_table%d" % h, tag="wide%d" % h, align_bytes=64) for h in range(HALVES)]
-        nc.sync.dma_start(out=gate_table[0][:], in_=tz[0:P, :])
-        list_gate = load_list("list_gate", offs6)
+        list_b = load_list("list_b", offs2)
         list_g = load_list("list_g", offs3)
-        nc.sync.dma_start(out=gate_table[1][:], in_=tz[P : 2 * P, :])
         pick_a = load_list("pick_a", offs4)
         pick_c = load_list("pick_c", offs5)
         ws_codes = load_words("ws_codes", ws_words, N)
@@ -83,19 +75,21 @@ def tile_list_triple_looked_skip_finalgate_kernel(
         load_scale_rows(nc, sx_plane, sx_scales)
         wb_codes = tile("wb_codes", [P, N], U16)
         nc.sync.dma_start(out=wb_codes[:].bitcast(I32), in_=wb_words[0].bitcast(I32))
+        list_gate = load_list("list_gate", offs6)
+        slope = tile("slope", [P, HALVES], F32)
+        offset = tile("offset", [P, HALVES], F32)
+        with nc.allow_non_contiguous_dma(reason="one value a partition"):
+            nc.sync.dma_start(out=slope[:], in_=so.rearrange("(h p) one -> p (h one)", p=P))
+            nc.sync.dma_start(out=offset[:], in_=bo.rearrange("(h p) one -> p (h one)", p=P))
+        gate_table = [tile("gate_table%d" % h, [P, E], F32) for h in range(HALVES)]
+        for h in range(HALVES):
+            nc.sync.dma_start(out=gate_table[h][:], in_=tz[h * P : (h + 1) * P, :])
         load_scale_rows(nc, wb_plane, wb_scales)
 
         w_codes_t = tile("w_codes_t", [P, PACK, P], U32)
         w_plane_t = tile("w_plane_t", [P, PACK, P], U8)
         nc.vector.tensor_copy(out=w_codes_t[:].rearrange("p t m -> p m t"), in_=w_codes[:].rearrange("p (m t) -> p m t", t=PACK))
         nc.vector.tensor_copy(out=w_plane_t[:].rearrange("p t m -> p m t"), in_=w_plane[:].rearrange("p (m t) -> p m t", t=PACK))
-
-        gate = [tile("gate%d" % h, [P, O], F32) for h in range(HALVES)]
-        for h in range(HALVES):
-            nc.scalar.activation(
-                out=gate[h][:], in_=gate_table[h][:].indirect(list_gate[:]), func=ACT.Sigmoid,
-                bias=offset[:, h : h + 1], scale=slope[:, h : h + 1],
-            )
 
         def first_product(name, offsets):
             codes = tile(name + "_codes", [P, J], U16)
@@ -118,9 +112,15 @@ def tile_list_triple_looked_skip_finalgate_kernel(
                 nc.scalar.copy(out=pairs[u][:], in_=banks[u][:])
             return pairs
 
-        a_pairs = to_sbuf("a", first_product("a", list_a), ("wide0", "a_pair1"))
+        a_pairs = to_sbuf("a", first_product("a", list_a), ("a_pair0", "a_pair1"))
         b_pairs = to_sbuf("b", first_product("b", list_b), ("b_pair0", "b_pair1"))
         g_banks = first_product("g", list_g)
+
+        a_picked = [tile("a_picked%d" % u, [P, 2, O], F32) for u in range(2)]
+        for v in range(2):
+            nc.vector.tensor_copy(out=a_picked[0][:, v, :], in_=a_pairs[0][:, v, :].indirect(pick_a[:]))
+        for v in range(2):
+            nc.scalar.activation(out=a_picked[1][:, v, :], in_=a_pairs[1][:, v, :].indirect(pick_a[:]), func=ACT.Copy)
 
         sums = [ps.tile([P, O], F32, name="sum%d" % h) for h in range(HALVES)]
         for h in range(HALVES):
@@ -131,21 +131,28 @@ def tile_list_triple_looked_skip_finalgate_kernel(
                 start=True, stop=False,
             )
 
-        a_picked = [tile("a_picked%d" % t, [P, O], F32) for t in range(PACK)]
-        for t in range(PACK):
-            nc.scalar.activation(out=a_picked[t][:], in_=a_pairs[t // 2][:, t % 2, :].indirect(pick_a[:]), func=ACT.Copy)
-
-        larger = [tile("larger%d" % t, [P, J], F32) for t in range(PACK)]
-        for t in range(PACK):
-            nc.vector.tensor_tensor(out=larger[t][:], in0=g_banks[t // 2][:, t % 2, :], in1=b_pairs[t // 2][:, t % 2, :], op=ALU.max)
-        diff = tile("diff", [P, PACK, O], F32)
-        for t in range(PACK):
-            nc.vector.tensor_tensor(out=diff[:, t, :], in0=larger[t][:].indirect(pick_c[:]), in1=a_picked[t][:], op=ALU.subtract)
+        larger_low = tile("larger_low", [P, 2, J], F32)
+        nc.vector.tensor_tensor(out=larger_low[:], in0=g_banks[0][:], in1=b_pairs[0][:], op=ALU.max)
+        larger_high = [tile("larger_high%d" % v, [P, J], F32) for v in range(2)]
+        for v in range(2):
+            nc.vector.tensor_tensor(out=larger_high[v][:], in0=g_banks[1][:, v, :], in1=b_pairs[1][:, v, :], op=ALU.max)
+        c_picked = tile("c_picked", [P, 2, O], F32)
+        for v in range(2):
+            nc.scalar.activation(out=c_picked[:, v, :], in_=larger_low[:, v, :].indirect(pick_c[:]), func=ACT.Copy)
+        diff = [tile("diff%d" % u, [P, 2, O], F32) for u in range(2)]
+        for v in range(2):
+            nc.vector.tensor_tensor(out=diff[1][:, v, :], in0=larger_high[v][:].indirect(pick_c[:]), in1=a_picked[1][:, v, :], op=ALU.subtract)
+        nc.vector.tensor_tensor(out=diff[0][:], in0=c_picked[:], in1=a_picked[0][:], op=ALU.subtract)
 
         hid = tile("hid", [P, O, PACK], BF16)
-        nc.scalar.activation(
-            out=hid[:].rearrange("p (c i) t -> p c t i", i=4), in_=diff[:].rearrange("p t (c i) -> p c t i", i=4), func=ACT.Abs,
-        )
+        for u in (1, 0):
+            nc.scalar.activation(out=hid[:, :, 2 * u : 2 * u + 2], in_=diff[u][:].rearrange("p v o -> p o v"), func=ACT.Abs)
+        gate = sb.tile([P, HALVES, O], F32, name="gate", tag="diff0", align_bytes=64)
+        for h in range(HALVES):
+            nc.scalar.activation(
+                out=gate[:, h, :], in_=gate_table[h][:].indirect(list_gate[:]), func=ACT.Sigmoid,
+                bias=offset[:, h : h + 1], scale=slope[:, h : h + 1],
+            )
         hid_codes = tile("hid_codes", [P, O], U32)
         hid_plane = tile("hid_plane", [P, O], U8)
         nc.vector.quantize_mx(out=hid_codes[:].bitcast(E5M2), scales=hid_plane[:], in_=hid[:].rearrange("p o t -> p (o t)"))
@@ -158,6 +165,6 @@ def tile_list_triple_looked_skip_finalgate_kernel(
                 start=False, stop=True,
             )
             result = tile("result%d" % h, [P, O], F32)
-            nc.vector.tensor_tensor(out=result[:], in0=sums[h][:], in1=gate[h][:], op=ALU.mult)
+            nc.vector.tensor_tensor(out=result[:], in0=sums[h][:], in1=gate[:, h, :], op=ALU.mult)
             queue = nc.sync if h == 0 else nc.scalar
             queue.dma_start(out=out[h * P : (h + 1) * P, :], in_=result[:])

@@ -57,6 +57,9 @@ def tile_list_triple_looked_skip_finalgate_kernel(
         wb_plane = tile("wb_plane", [P, N], U8)
 
         nc.vector.memset(xt_plane[:].bitcast(I32), 0)
+        warm = tile("warm", [P, 2], F32)
+        nc.gpsimd.memset(warm[:, 0:1], 0.0)
+        nc.scalar.activation(out=warm[:, 1:2], in_=warm[:, 0:1], func=ACT.Sigmoid)
         load_scale_rows(nc, w_plane, w_scales, range(3))
         w_codes = load_words("w_codes", w_words, R)
         load_scale_rows(nc, w_plane, w_scales, range(3, 4))

@@ -19,10 +19,12 @@ ALU = mybir.AluOpType
 
 P = 128
 PACK = 4
+QUADRANTS = 4
 HALVES = N // P
+LOW, HIGH = (0, 1), (2, 3)
 
 
-def load_scale_rows(nc, plane, scales, quadrants=range(4)):
+def load_scale_rows(nc, plane, scales, quadrants=range(QUADRANTS)):
     for q in quadrants:
         rows = scales[0, 4 * q : 4 * q + 4, :].bitcast(I32)
         nc.sync.dma_start(out=plane[32 * q : 32 * q + 32, :].bitcast(I32), in_=rows.unsqueeze(0).to_broadcast([8] + list(rows.shape)))
@@ -45,9 +47,14 @@ def tile_list_triple_looked_skip_finalgate_kernel(
             nc.sync.dma_start(offsets[:], source)
             return offsets
 
-        def load_words(name, source, width):
+        def load_e4m3_words(name, source, width):
             words = tile(name, [P, width], U32)
             nc.sync.dma_start(out=words[:].bitcast(I32), in_=source[0].rearrange("p c r -> p (c r)").bitcast(I32))
+            return words
+
+        def load_e2m1_words(name, source, width):
+            words = tile(name, [P, width], U16)
+            nc.sync.dma_start(out=words[:].bitcast(I32), in_=source[0].bitcast(I32))
             return words
 
         w_plane = tile("w_plane", [P, R], U8)
@@ -57,31 +64,31 @@ def tile_list_triple_looked_skip_finalgate_kernel(
         wb_plane = tile("wb_plane", [P, N], U8)
 
         nc.vector.memset(xt_plane[:].bitcast(I32), 0)
+
         warm = tile("warm", [P, 2], F32)
         nc.gpsimd.memset(warm[:, 0:1], 0.0)
         nc.scalar.activation(out=warm[:, 1:2], in_=warm[:, 0:1], func=ACT.Sigmoid)
-        load_scale_rows(nc, w_plane, w_scales, range(3))
-        w_codes = load_words("w_codes", w_words, R)
-        load_scale_rows(nc, w_plane, w_scales, range(3, 4))
-        xt_codes = tile("xt_codes", [P, T], U16)
-        nc.sync.dma_start(out=xt_codes[:].bitcast(I32), in_=xt_words[0].bitcast(I32))
+
+        load_scale_rows(nc, w_plane, w_scales, range(0, 2))
+        w_codes = load_e4m3_words("w_codes", w_words, R)
+        load_scale_rows(nc, w_plane, w_scales, range(2, QUADRANTS))
+        xt_codes = load_e2m1_words("xt_codes", xt_words, T)
         list_a = load_list("list_a", offs)
-        for q in range(4):
-            nc.sync.dma_start(out=xt_plane[32 * q : 32 * q + 4, :].bitcast(I32), in_=xt_scales[0, 4 * q : 4 * q + 4, :].bitcast(I32))
+        for q, queue in enumerate((nc.sync, nc.sync, nc.sync, nc.gpsimd)):
+            queue.dma_start(out=xt_plane[32 * q : 32 * q + 4, :].bitcast(I32), in_=xt_scales[0, 4 * q : 4 * q + 4, :].bitcast(I32))
         list_b = load_list("list_b", offs2)
         list_g = load_list("list_g", offs3)
         pick_a = load_list("pick_a", offs4)
         pick_c = load_list("pick_c", offs5)
-        ws_codes = load_words("ws_codes", ws_words, N)
-        sx_codes = load_words("sx_codes", sx_words, O)
+        ws_codes = load_e4m3_words("ws_codes", ws_words, N)
+        sx_codes = load_e4m3_words("sx_codes", sx_words, O)
         load_scale_rows(nc, ws_plane, ws_scales)
         load_scale_rows(nc, sx_plane, sx_scales)
-        wb_codes = tile("wb_codes", [P, N], U16)
-        nc.sync.dma_start(out=wb_codes[:].bitcast(I32), in_=wb_words[0].bitcast(I32))
+        wb_codes = load_e2m1_words("wb_codes", wb_words, N)
         list_gate = load_list("list_gate", offs6)
         slope = tile("slope", [P, HALVES], F32)
         offset = tile("offset", [P, HALVES], F32)
-        with nc.allow_non_contiguous_dma(reason="one value a partition"):
+        with nc.allow_non_contiguous_dma(reason="one value a partition for each half of the output features"):
             nc.sync.dma_start(out=slope[:], in_=so.rearrange("(h p) one -> p (h one)", p=P))
             nc.sync.dma_start(out=offset[:], in_=bo.rearrange("(h p) one -> p (h one)", p=P))
         gate_table = [tile("gate_table%d" % h, [P, E], F32) for h in range(HALVES)]
@@ -94,38 +101,41 @@ def tile_list_triple_looked_skip_finalgate_kernel(
         nc.vector.tensor_copy(out=w_codes_t[:].rearrange("p t m -> p m t"), in_=w_codes[:].rearrange("p (m t) -> p m t", t=PACK))
         nc.vector.tensor_copy(out=w_plane_t[:].rearrange("p t m -> p m t"), in_=w_plane[:].rearrange("p (m t) -> p m t", t=PACK))
 
-        def first_product(name, offsets):
-            codes = tile(name + "_codes", [P, J], U16)
-            plane = tile(name + "_plane", [P, J], U8)
-            nc.vector.tensor_copy(out=codes[:], in_=xt_codes[:].indirect(offsets[:]))
-            nc.vector.tensor_copy(out=plane[:], in_=xt_plane[:].indirect(offsets[:]))
-            banks = [ps.tile([P, 2, J], F32, name="%s_bank%d" % (name, u)) for u in range(2)]
+        def gathered(name, dtype, window, offsets):
+            picked = tile(name, [P, J], dtype)
+            nc.vector.tensor_copy(out=picked[:], in_=window[:].indirect(offsets[:]))
+            return picked
+
+        a_codes = gathered("a_codes", U16, xt_codes, list_a)
+        a_plane = gathered("a_plane", U8, xt_plane, list_a)
+        b_codes = gathered("b_codes", U16, xt_codes, list_b)
+        b_plane = gathered("b_plane", U8, xt_plane, list_b)
+        g_codes = gathered("g_codes", U16, xt_codes, list_g)
+        g_plane = gathered("g_plane", U8, xt_plane, list_g)
+
+        def first_product(codes, plane, slices):
             for t in range(PACK):
                 nc.tensor.matmul_mx(
-                    out=banks[t // 2][:, t % 2, :],
+                    out=slices[t],
                     lhsT=w_codes_t[:, t, :].bitcast(E4M3), lhsT_scale=w_plane_t[:, t, :],
                     rhs=codes[:].bitcast(E2M1), rhs_scale=plane[:],
                     start=True, stop=True,
                 )
-            return banks
 
-        def to_sbuf(name, banks, tags):
-            pairs = [sb.tile([P, 2, J], F32, name="%s_pair%d" % (name, u), tag=tags[u], align_bytes=64) for u in range(2)]
+        def product_to_sbuf(name, codes, plane):
+            banks = [ps.tile([P, 2, J], F32, name="%s_bank%d" % (name, u)) for u in range(2)]
+            first_product(codes, plane, [banks[t // 2][:, t % 2, :] for t in range(PACK)])
+            whole = tile(name + "_whole", [P, PACK, J], F32)
             for u in range(2):
-                nc.scalar.copy(out=pairs[u][:], in_=banks[u][:])
-            return pairs
+                nc.scalar.copy(out=whole[:, 2 * u : 2 * u + 2, :], in_=banks[u][:])
+            return whole
 
-        a_pairs = to_sbuf("a", first_product("a", list_a), ("a_pair0", "a_pair1"))
-        b_pairs = to_sbuf("b", first_product("b", list_b), ("b_pair0", "b_pair1"))
-        g_banks = first_product("g", list_g)
+        a_whole = product_to_sbuf("a", a_codes, a_plane)
+        b_whole = product_to_sbuf("b", b_codes, b_plane)
+        g_banks = [ps.tile([P, J], F32, name="g_bank%d" % t) for t in range(PACK)]
+        first_product(g_codes, g_plane, [bank[:] for bank in g_banks])
 
-        a_picked = [tile("a_picked%d" % u, [P, 2, O], F32) for u in range(2)]
-        for v in range(2):
-            nc.vector.tensor_copy(out=a_picked[0][:, v, :], in_=a_pairs[0][:, v, :].indirect(pick_a[:]))
-        for v in range(2):
-            nc.scalar.activation(out=a_picked[1][:, v, :], in_=a_pairs[1][:, v, :].indirect(pick_a[:]), func=ACT.Copy)
-
-        sums = [ps.tile([P, O], F32, name="sum%d" % h) for h in range(HALVES)]
+        sums = [ps.tile([P, O], F32, name="sum%d" % h, tag="a_bank%d" % h) for h in range(HALVES)]
         for h in range(HALVES):
             nc.tensor.matmul_mx(
                 out=sums[h][:],
@@ -134,23 +144,28 @@ def tile_list_triple_looked_skip_finalgate_kernel(
                 start=True, stop=False,
             )
 
-        larger_low = tile("larger_low", [P, 2, J], F32)
-        nc.vector.tensor_tensor(out=larger_low[:], in0=g_banks[0][:], in1=b_pairs[0][:], op=ALU.max)
-        larger_high = [tile("larger_high%d" % v, [P, J], F32) for v in range(2)]
-        for v in range(2):
-            nc.vector.tensor_tensor(out=larger_high[v][:], in0=g_banks[1][:, v, :], in1=b_pairs[1][:, v, :], op=ALU.max)
-        c_picked = tile("c_picked", [P, 2, O], F32)
-        for v in range(2):
-            nc.scalar.activation(out=c_picked[:, v, :], in_=larger_low[:, v, :].indirect(pick_c[:]), func=ACT.Copy)
-        diff = [tile("diff%d" % u, [P, 2, O], F32) for u in range(2)]
-        for v in range(2):
-            nc.vector.tensor_tensor(out=diff[1][:, v, :], in0=larger_high[v][:].indirect(pick_c[:]), in1=a_picked[1][:, v, :], op=ALU.subtract)
-        nc.vector.tensor_tensor(out=diff[0][:], in0=c_picked[:], in1=a_picked[0][:], op=ALU.subtract)
+        a_picked = tile("a_picked", [P, PACK, O], F32)
+        for t in LOW:
+            nc.vector.tensor_copy(out=a_picked[:, t, :], in_=a_whole[:, t, :].indirect(pick_a[:]))
+        for t in HIGH:
+            nc.scalar.activation(out=a_picked[:, t, :], in_=a_whole[:, t, :].indirect(pick_a[:]), func=ACT.Copy)
+
+        larger = [tile("larger%d" % t, [P, J], F32) for t in range(PACK)]
+        for t in range(PACK):
+            nc.vector.tensor_tensor(out=larger[t][:], in0=g_banks[t][:], in1=b_whole[:, t, :], op=ALU.max)
+        c_picked = tile("c_picked", [P, len(LOW), O], F32)
+        for t in LOW:
+            nc.scalar.activation(out=c_picked[:, t, :], in_=larger[t][:].indirect(pick_c[:]), func=ACT.Copy)
+        diff = tile("diff", [P, PACK, O], F32)
+        for t in HIGH:
+            nc.vector.tensor_tensor(out=diff[:, t, :], in0=larger[t][:].indirect(pick_c[:]), in1=a_picked[:, t, :], op=ALU.subtract)
+        nc.vector.tensor_tensor(out=diff[:, 0:2, :], in0=c_picked[:], in1=a_picked[:, 0:2, :], op=ALU.subtract)
 
         hid = tile("hid", [P, O, PACK], BF16)
-        for u in (1, 0):
-            nc.scalar.activation(out=hid[:, :, 2 * u : 2 * u + 2], in_=diff[u][:].rearrange("p v o -> p o v"), func=ACT.Abs)
-        gate = sb.tile([P, HALVES, O], F32, name="gate", tag="diff0", align_bytes=64)
+        for first, last in (HIGH, LOW):
+            nc.scalar.activation(out=hid[:, :, first : last + 1], in_=diff[:, first : last + 1, :].rearrange("p v o -> p o v"), func=ACT.Abs)
+
+        gate = sb.tile([P, HALVES, O], F32, name="gate", tag="diff", align_bytes=64)
         for h in range(HALVES):
             nc.scalar.activation(
                 out=gate[:, h, :], in_=gate_table[h][:].indirect(list_gate[:]), func=ACT.Sigmoid,
@@ -169,5 +184,4 @@ def tile_list_triple_looked_skip_finalgate_kernel(
             )
             result = tile("result%d" % h, [P, O], F32)
             nc.vector.tensor_tensor(out=result[:], in0=sums[h][:], in1=gate[:, h, :], op=ALU.mult)
-            queue = nc.sync if h == 0 else nc.scalar
-            queue.dma_start(out=out[h * P : (h + 1) * P, :], in_=result[:])
+            (nc.sync, nc.scalar)[h].dma_start(out=out[h * P : (h + 1) * P, :], in_=result[:])

from contextlib import ExitStack

import concourse.mybir as mybir

K, T, J, R, O, N, L, E = 512, 2048, 256, 512, 128, 256, 512, 512
FLOPS = 2 * K * R * 3 * J + 2 * R * N * O + 2 * L * N * O

F32 = mybir.dt.float32
BF16 = mybir.dt.bfloat16
I32 = mybir.dt.int32
U32 = mybir.dt.uint32
U16 = mybir.dt.uint16
U8 = mybir.dt.uint8
E4M3 = mybir.dt.float8_e4m3fn_x4
E5M2 = mybir.dt.float8_e5m2_x4
E2M1 = mybir.dt.float4_e2m1fn_x4
ACT = mybir.ActivationFunctionType
ALU = mybir.AluOpType

P = 128
PACK = 4
QUADRANTS = 4
HALVES = N // P
LOW, HIGH = (0, 1), (2, 3)


def load_scale_rows(nc, plane, scales, quadrants=range(QUADRANTS)):
    for q in quadrants:
        rows = scales[0, 4 * q : 4 * q + 4, :].bitcast(I32)
        nc.sync.dma_start(out=plane[32 * q : 32 * q + 32, :].bitcast(I32), in_=rows.unsqueeze(0).to_broadcast([8] + list(rows.shape)))


def tile_list_triple_looked_skip_finalgate_kernel(
    tc, xt_words, xt_scales, w_words, w_scales, wb_words, wb_scales, sx_words, sx_scales, ws_words, ws_scales,
    tz, so, bo, offs, offs2, offs3, offs4, offs5, offs6, out,
):
    nc = tc.nc
    with ExitStack() as ctx:
        sb = ctx.enter_context(tc.tile_pool(name="sb", bufs=1))
        ps = ctx.enter_context(tc.psum_pool(name="ps", bufs=1))

        def tile(name, shape, dtype):
            return sb.tile(shape, dtype, name=name, align_bytes=64)

        def load_list(name, source):
            offsets = tile(name, list(source.shape), U16)
            nc.sync.dma_start(offsets[:], source)
            return offsets

        def load_e4m3_words(name, source, width):
            words = tile(name, [P, width], U32)
            nc.sync.dma_start(out=words[:].bitcast(I32), in_=source[0].rearrange("p c r -> p (c r)").bitcast(I32))
            return words

        def load_e2m1_words(name, source, width):
            words = tile(name, [P, width], U16)
            nc.sync.dma_start(out=words[:].bitcast(I32), in_=source[0].bitcast(I32))
            return words

        w_plane = tile("w_plane", [P, R], U8)
        xt_plane = tile("xt_plane", [P, T], U8)
        ws_plane = tile("ws_plane", [P, N], U8)
        sx_plane = tile("sx_plane", [P, O], U8)
        wb_plane = tile("wb_plane", [P, N], U8)

        nc.vector.memset(xt_plane[:].bitcast(I32), 0)

        warm = tile("warm", [P, 2], F32)
        nc.gpsimd.memset(warm[:, 0:1], 0.0)
        nc.scalar.activation(out=warm[:, 1:2], in_=warm[:, 0:1], func=ACT.Sigmoid)

        load_scale_rows(nc, w_plane, w_scales, range(0, 2))
        w_codes = load_e4m3_words("w_codes", w_words, R)
        load_scale_rows(nc, w_plane, w_scales, range(2, QUADRANTS))
        xt_codes = load_e2m1_words("xt_codes", xt_words, T)
        list_a = load_list("list_a", offs)
        for q, queue in enumerate((nc.sync, nc.sync, nc.sync, nc.gpsimd)):
            queue.dma_start(out=xt_plane[32 * q : 32 * q + 4, :].bitcast(I32), in_=xt_scales[0, 4 * q : 4 * q + 4, :].bitcast(I32))
        list_b = load_list("list_b", offs2)
        list_g = load_list("list_g", offs3)
        pick_a = load_list("pick_a", offs4)
        pick_c = load_list("pick_c", offs5)
        ws_codes = load_e4m3_words("ws_codes", ws_words, N)
        sx_codes = load_e4m3_words("sx_codes", sx_words, O)
        load_scale_rows(nc, ws_plane, ws_scales)
        load_scale_rows(nc, sx_plane, sx_scales)
        wb_codes = load_e2m1_words("wb_codes", wb_words, N)
        list_gate = load_list("list_gate", offs6)
        slope = tile("slope", [P, HALVES], F32)
        offset = tile("offset", [P, HALVES], F32)
        with nc.allow_non_contiguous_dma(reason="one value a partition for each half of the output features"):
            nc.sync.dma_start(out=slope[:], in_=so.rearrange("(h p) one -> p (h one)", p=P))
            nc.sync.dma_start(out=offset[:], in_=bo.rearrange("(h p) one -> p (h one)", p=P))
        gate_table = [tile("gate_table%d" % h, [P, E], F32) for h in range(HALVES)]
        for h in range(HALVES):
            nc.sync.dma_start(out=gate_table[h][:], in_=tz[h * P : (h + 1) * P, :])
        load_scale_rows(nc, wb_plane, wb_scales)

        w_codes_t = tile("w_codes_t", [P, PACK, P], U32)
        w_plane_t = tile("w_plane_t", [P, PACK, P], U8)
        nc.vector.tensor_copy(out=w_codes_t[:].rearrange("p t m -> p m t"), in_=w_codes[:].rearrange("p (m t) -> p m t", t=PACK))
        nc.vector.tensor_copy(out=w_plane_t[:].rearrange("p t m -> p m t"), in_=w_plane[:].rearrange("p (m t) -> p m t", t=PACK))

        def gathered(name, dtype, window, offsets):
            picked = tile(name, [P, J], dtype)
            nc.vector.tensor_copy(out=picked[:], in_=window[:].indirect(offsets[:]))
            return picked

        a_codes = gathered("a_codes", U16, xt_codes, list_a)
        a_plane = gathered("a_plane", U8, xt_plane, list_a)
        b_codes = gathered("b_codes", U16, xt_codes, list_b)
        b_plane = gathered("b_plane", U8, xt_plane, list_b)
        g_codes = gathered("g_codes", U16, xt_codes, list_g)
        g_plane = gathered("g_plane", U8, xt_plane, list_g)

        def first_product(codes, plane, slices):
            for t in range(PACK):
                nc.tensor.matmul_mx(
                    out=slices[t],
                    lhsT=w_codes_t[:, t, :].bitcast(E4M3), lhsT_scale=w_plane_t[:, t, :],
                    rhs=codes[:].bitcast(E2M1), rhs_scale=plane[:],
                    start=True, stop=True,
                )

        def product_to_sbuf(name, codes, plane):
            banks = [ps.tile([P, 2, J], F32, name="%s_bank%d" % (name, u)) for u in range(2)]
            first_product(codes, plane, [banks[t // 2][:, t % 2, :] for t in range(PACK)])
            whole = tile(name + "_whole", [P, PACK, J], F32)
            for u in range(2):
                nc.scalar.copy(out=whole[:, 2 * u : 2 * u + 2, :], in_=banks[u][:])
            return whole

        a_whole = product_to_sbuf("a", a_codes, a_plane)
        b_whole = product_to_sbuf("b", b_codes, b_plane)
        g_banks = [ps.tile([P, J], F32, name="g_bank%d" % t) for t in range(PACK)]
        first_product(g_codes, g_plane, [bank[:] for bank in g_banks])

        sums = [ps.tile([P, O], F32, name="sum%d" % h, tag="a_bank%d" % h) for h in range(HALVES)]
        for h in range(HALVES):
            nc.tensor.matmul_mx(
                out=sums[h][:],
                lhsT=ws_codes[:, h * P : (h + 1) * P].bitcast(E4M3), lhsT_scale=ws_plane[:, h * P : (h + 1) * P],
                rhs=sx_codes[:].bitcast(E4M3), rhs_scale=sx_plane[:],
                start=True, stop=False,
            )

        a_picked = tile("a_picked", [P, PACK, O], F32)
        for t in LOW:
            nc.vector.tensor_copy(out=a_picked[:, t, :], in_=a_whole[:, t, :].indirect(pick_a[:]))
        for t in HIGH:
            nc.scalar.activation(out=a_picked[:, t, :], in_=a_whole[:, t, :].indirect(pick_a[:]), func=ACT.Copy)

        larger = [tile("larger%d" % t, [P, J], F32) for t in range(PACK)]
        for t in range(PACK):
            nc.vector.tensor_tensor(out=larger[t][:], in0=g_banks[t][:], in1=b_whole[:, t, :], op=ALU.max)
        c_picked = tile("c_picked", [P, len(LOW), O], F32)
        for t in LOW:
            nc.scalar.activation(out=c_picked[:, t, :], in_=larger[t][:].indirect(pick_c[:]), func=ACT.Copy)
        diff = tile("diff", [P, PACK, O], F32)
        for t in HIGH:
            nc.vector.tensor_tensor(out=diff[:, t, :], in0=larger[t][:].indirect(pick_c[:]), in1=a_picked[:, t, :], op=ALU.subtract)
        nc.vector.tensor_tensor(out=diff[:, 0:2, :], in0=c_picked[:], in1=a_picked[:, 0:2, :], op=ALU.subtract)

        hid = tile("hid", [P, O, PACK], BF16)
        for first, last in (HIGH, LOW):
            nc.scalar.activation(out=hid[:, :, first : last + 1], in_=diff[:, first : last + 1, :].rearrange("p v o -> p o v"), func=ACT.Abs)

        gate = sb.tile([P, HALVES, O], F32, name="gate", tag="diff", align_bytes=64)
        for h in range(HALVES):
            nc.scalar.activation(
                out=gate[:, h, :], in_=gate_table[h][:].indirect(list_gate[:]), func=ACT.Sigmoid,
                bias=offset[:, h : h + 1], scale=slope[:, h : h + 1],
            )
        hid_codes = tile("hid_codes", [P, O], U32)
        hid_plane = tile("hid_plane", [P, O], U8)
        nc.vector.quantize_mx(out=hid_codes[:].bitcast(E5M2), scales=hid_plane[:], in_=hid[:].rearrange("p o t -> p (o t)"))

        for h in range(HALVES):
            nc.tensor.matmul_mx(
                out=sums[h][:],
                lhsT=wb_codes[:, h * P : (h + 1) * P].bitcast(E2M1), lhsT_scale=wb_plane[:, h * P : (h + 1) * P],
                rhs=hid_codes[:].bitcast(E5M2), rhs_scale=hid_plane[:],
                start=False, stop=True,
            )
            result = tile("result%d" % h, [P, O], F32)
            nc.vector.tensor_tensor(out=result[:], in0=sums[h][:], in1=gate[:, h, :], op=ALU.mult)
            (nc.sync, nc.scalar)[h].dma_start(out=out[h * P : (h + 1) * P, :], in_=result[:])
